import numpy as np
import ml_dtypes


def mxq(x, axis, fmt="e4m3"):
    dtype, down = {"e4m3": (ml_dtypes.float8_e4m3fn, 7), "e5m2": (ml_dtypes.float8_e5m2, 14)}[fmt]
    v = np.moveaxis(np.asarray(x, np.float32).astype(ml_dtypes.bfloat16).astype(np.float64), axis, -1)
    blocks = v.reshape(v.shape[:-1] + (-1, 32))
    amax = np.abs(blocks).max(-1, keepdims=True)
    byte = np.maximum(np.where(amax > 0, np.frexp(amax)[1] - 1 + 127, 0) - down, 1)
    scale = np.exp2(byte - 127.0)
    codes = (blocks / scale).astype(np.float32).astype(dtype).astype(np.float64)
    return np.moveaxis((codes * scale).reshape(v.shape), -1, axis)


WIDE = False


def mx_kscale(k):
    if not WIDE:
        return np.ones(k)
    levels = np.array([10, -10, 5, -5, 0])
    if k % 512:
        return np.exp2(np.random.permutation(np.resize(levels, k // 32))).repeat(32)
    a = np.empty((k // 512, 16))
    for p in range(k // 512):
        a[p, :8] = np.random.permutation(np.resize(levels, 8))
        for g in range(8):
            far = levels[np.abs(levels - a[p, g]) >= 10]
            a[p, g + 8] = far[np.random.randint(len(far))]
    return np.exp2(a.ravel()).repeat(32)


def f64(x):
    return np.asarray(x).astype(np.float64)


def striped(idx):
    return np.tile(idx.reshape(-1, 16).T, (8, 1)).astype(np.uint16)


def unstriped(offs):
    return offs[:16].T.reshape(-1).astype(np.int64)


def striped8(idx):
    return np.concatenate([x.reshape(-1, 16).T for x in idx]).astype(np.uint16)


def runs(offs, k):
    lists = np.stack([offs[16 * r : 16 * r + 16].T.reshape(-1) for r in range(8)]).astype(np.int64)
    return lists[np.arange(k) % 512 // 64]


def pack_weight(w):
    k, n = w.shape
    w = f64(np.asarray(w, np.float32).astype(ml_dtypes.bfloat16)).reshape(k // 32, 32, n)
    amax = np.abs(w).max(1)
    byte = np.clip(np.where(amax > 0, np.frexp(amax)[1] - 1 + 127 - 7, 1), 1, 254)
    scaled = (w * np.exp2(127.0 - byte)[:, None, :]).reshape(k, n).astype(np.float32)
    words = np.ascontiguousarray(scaled.reshape(k // 512, 128, 4, n).transpose(0, 1, 3, 2)).astype(ml_dtypes.float8_e4m3fn).view(np.uint8)
    return words, np.ascontiguousarray(byte.astype(np.uint8).reshape(k // 512, 16, n))


def unpack_weight(words, scales):
    g, p, n, _ = words.shape
    vals = np.ascontiguousarray(words).view(ml_dtypes.float8_e4m3fn).astype(np.float64) * np.repeat(np.exp2(scales.astype(np.float64) - 127.0), 8, axis=1)[..., None]
    return vals.transpose(0, 1, 3, 2).reshape(g * 512, n)


E2M1 = np.array([0.0, 0.5, 1.0, 1.5, 2.0, 3.0, 4.0, 6.0, -0.0, -0.5, -1.0, -1.5, -2.0, -3.0, -4.0, -6.0])


def pack_fp4(w):
    k, n = w.shape
    w = f64(np.asarray(w, np.float32).astype(ml_dtypes.bfloat16)).reshape(k // 32, 32, n)
    amax = np.abs(w).max(1)
    mant, ex = np.frexp(amax / 6.0)
    byte = np.clip(np.where(amax > 0, np.where(mant > 0.5, ex, ex - 1) + 127, 1), 1, 254)
    scaled = (w * np.exp2(127.0 - byte)[:, None, :]).reshape(k, n).astype(np.float32)
    c = np.ascontiguousarray(scaled.reshape(k // 512, 128, 4, n).transpose(0, 1, 3, 2)).astype(ml_dtypes.float4_e2m1fn).view(np.uint8) & 0xF
    words = (c[..., 0::2] | (c[..., 1::2] << 4)).reshape(k // 512, 128, 2 * n)
    return np.ascontiguousarray(words), np.ascontiguousarray(byte.astype(np.uint8).reshape(k // 512, 16, n))


def unpack_fp4(words, scales):
    g, _, n = scales.shape
    words = np.ascontiguousarray(words).reshape(g, 128, n, 2)
    nib = np.empty((g, 128, n, 4), np.uint8)
    nib[..., 0::2] = words & 0xF
    nib[..., 1::2] = words >> 4
    vals = E2M1[nib] * np.repeat(np.exp2(scales.astype(np.float64) - 127.0), 8, axis=1)[..., None]
    return vals.transpose(0, 1, 3, 2).reshape(g * 512, n)


def sigmoid(v):
    return 1.0 / (1.0 + np.exp(-np.maximum(v, -700.0)))

def planes(y):
    n, m = y.shape
    v = y.astype(np.float32).astype(ml_dtypes.bfloat16).astype(np.float64).reshape(n // 32, 32, m)
    top = np.abs(v).max(1)
    byte = np.clip(np.where(top > 0, np.frexp(top)[1] - 1 + 127 - 7, 1), 1, 254)
    codes = (v * np.exp2(127.0 - byte)[:, None, :]).reshape(n, m).astype(np.float32).astype(ml_dtypes.float8_e4m3fn).view(np.uint8)
    words = codes.reshape(n // 512, 128, 4, m).transpose(0, 1, 3, 2)
    return np.ascontiguousarray(words), np.ascontiguousarray(byte.astype(np.uint8).reshape(n // 512, 16, m))


K, T, S, H = 512, 2048, 512, 512


def setup_inputs():
    n = np.random.standard_normal
    s = mx_kscale(K)[:, None]
    u = mx_kscale(H)
    packed_xT = pack_weight(n((K, T)) * s)
    packed_w1 = pack_fp4(n((K, H)) / np.sqrt(K) / s)
    packed_w2 = pack_fp4(n((H, H)) / np.sqrt(H) / u[:, None])
    return {
        "x_words": packed_xT[0],
        "x_scales": packed_xT[1],
        "w1_words": packed_w1[0],
        "w1_scales": packed_w1[1],
        "gn": (np.random.uniform(0.5, 1.5, (H, 1)) * u[:, None]).astype(np.float32),
        "w2_words": packed_w2[0],
        "w2_scales": packed_w2[1],
        "offs": striped(np.random.permutation(T)[:S]),
        "n1": striped8(np.stack([np.random.permutation(S) for _ in range(8)])),
        "n2": striped8(np.stack([np.random.permutation(S) for _ in range(8)])),
        "n3": striped8(np.stack([np.random.permutation(S) for _ in range(8)])),
        "n4": striped8(np.stack([np.random.permutation(S) for _ in range(8)])),
        "n5": striped8(np.stack([np.random.permutation(S) for _ in range(8)])),
        "n6": striped8(np.stack([np.random.permutation(S) for _ in range(8)])),
    }


def reference(x_words, x_scales, w1_words, w1_scales, gn, w2_words, w2_scales, offs, n1, n2, n3, n4, n5, n6):
    xq = unpack_weight(x_words, x_scales)[:, unstriped(offs)]
    y = unpack_fp4(w1_words, w1_scales).T @ xq
    z = f64(gn) * (0.75 * (y[np.arange(H)[:, None], runs(n1, H)] + y[np.arange(H)[:, None], runs(n2, H)]) - y)
    w2q = unpack_fp4(w2_words, w2_scales)
    a = w2q.T @ mxq(z, 0, "e4m3")
    z2 = f64(gn) * (y - (np.minimum(y[np.arange(H)[:, None], runs(n3, H)], y[np.arange(H)[:, None], runs(n4, H)])))
    b = w2q.T @ mxq(z2, 0, "e4m3")
    out_0 = a + (sigmoid(b[np.arange(H)[:, None], runs(n6, H)] - b)) * (a[np.arange(H)[:, None], runs(n5, H)] - a)
    return (out_0,) + planes(out_0)

@@ -1,0 +1,224 @@
+from contextlib import ExitStack
+
+import concourse.mybir as mybir
+
+F32 = mybir.dt.float32
+BF16 = mybir.dt.bfloat16
+I32 = mybir.dt.int32
+U32 = mybir.dt.uint32
+U16 = mybir.dt.uint16
+U8 = mybir.dt.uint8
+E4M3X4 = mybir.dt.float8_e4m3fn_x4
+E2M1X4 = mybir.dt.float4_e2m1fn_x4
+ALU = mybir.AluOpType
+ACT = mybir.ActivationFunctionType
+
+P = 128
+PACK = 4
+T = 2048
+S = 512
+H = 512
+HALF = S // 2
+FLOPS = 3 * 2 * 512 * 512 * 512
+
+
+def tile_picked_tiepullblapunder_none_po_kernel(
+    tc, x_words, x_scales, w1_words, w1_scales, gn, w2_words, w2_scales, offs, n1, n2, n3, n4, n5, n6, out_0, out_1, out_2
+):
+    nc = tc.nc
+    with ExitStack() as ctx:
+        lists = ctx.enter_context(tc.tile_pool(name="lists", bufs=1))
+        sb = ctx.enter_context(tc.tile_pool(name="sb", bufs=1))
+        ps = ctx.enter_context(tc.psum_pool(name="ps", bufs=1))
+
+        def load_list(src, name):
+            tl = lists.tile([P, S // 16], U16, name=name)
+            nc.sync.dma_start(tl[:], src)
+            return tl
+
+        def load_scale_rows(queue, dst, src):
+            for q in range(4):
+                queue.dma_start(dst[32 * q : 32 * q + 4, :].bitcast(I32), src[0, 4 * q : 4 * q + 4, :].bitcast(I32))
+
+        xs_raw = sb.tile([P, T // 4], I32, name="xs_raw", align_bytes=64)
+        w1s_raw = sb.tile([P, H // 4], I32, name="w1s_raw", align_bytes=64)
+        w2s_raw = sb.tile([P, H // 4], I32, name="w2s_raw", align_bytes=64)
+        nc.gpsimd.memset(xs_raw[:], 0)
+        nc.gpsimd.memset(w1s_raw[:], 0)
+        nc.gpsimd.memset(w2s_raw[:], 0)
+
+        offs_t = load_list(offs, "offs_t")
+        load_scale_rows(nc.scalar, xs_raw[:].bitcast(U8), x_scales)
+        xw_raw = sb.tile([P, T], I32, name="xw_raw", align_bytes=64)
+        nc.sync.dma_start(xw_raw[:], x_words[0].rearrange("p c r -> p (c r)").bitcast(I32))
+        w1w_raw = sb.tile([P, H // 2], I32, name="w1w_raw", align_bytes=64)
+        nc.sync.dma_start(w1w_raw[:], w1_words[0].bitcast(I32))
+        load_scale_rows(nc.sync, w1s_raw[:].bitcast(U8), w1_scales)
+        n3_t = load_list(n3, "n3_t")
+        n4_t = load_list(n4, "n4_t")
+        gain = sb.tile([P, PACK], F32, name="gain")
+        nc.sync.dma_start(gain[:], gn.rearrange("(p t) o -> p (t o)", t=PACK))
+        w2w_raw = sb.tile([P, H // 2], I32, name="w2w_raw", align_bytes=64)
+        nc.sync.dma_start(w2w_raw[:], w2_words[0].bitcast(I32))
+        load_scale_rows(nc.sync, w2s_raw[:].bitcast(U8), w2_scales)
+        n1_t = load_list(n1, "n1_t")
+        n2_t = load_list(n2, "n2_t")
+        n6_t = load_list(n6, "n6_t")
+        n5_t = load_list(n5, "n5_t")
+        gain34 = sb.tile([P, PACK], F32, name="gain34")
+        nc.gpsimd.tensor_scalar(gain34[:], gain[:], 0.75, 0.0, ALU.mult, ALU.add)
+
+
+        def deal_words(raw, name):
+            dealt = sb.tile([P, 2 * H], U8, name=name, align_bytes=64)
+            nc.vector.tensor_copy(
+                dealt[:].rearrange("p (t m b) -> p t m b", t=PACK, b=2),
+                raw[:].bitcast(U8).rearrange("p (m t b) -> p t m b", t=PACK, b=2),
+            )
+            return dealt
+
+        def deal_scales(raw, name):
+            dealt = sb.tile([P, H], U8, name=name, align_bytes=64)
+            nc.vector.tensor_copy(
+                dealt[:].rearrange("p (t m) -> p t m", t=PACK),
+                raw[:].bitcast(U8).rearrange("p (m t) -> p t m", t=PACK),
+            )
+            return dealt
+
+        w1w = deal_words(w1w_raw, "w1w")
+        xs = sb.tile([P, S], U8, name="xs", align_bytes=64)
+        nc.vector.tensor_copy(xs[:], xs_raw[:].bitcast(U8).indirect(offs_t[:]))
+        w1s = deal_scales(w1s_raw, "w1s")
+        xw = sb.tile([P, S], U32, name="xw", align_bytes=64)
+        nc.vector.tensor_copy(xw[:], xw_raw[:].bitcast(U32).indirect(offs_t[:]))
+
+        def product(ww, ws, codes, scales, tag):
+            banks = []
+            for t in range(PACK):
+                bank = ps.tile([P, S], F32, name="bank_%s%d" % (tag, t), tag="bank_%s%d" % (tag, t))
+                nc.tensor.matmul_mx(
+                    out=bank[:],
+                    lhsT=ww[:, 2 * P * t : 2 * P * (t + 1)].bitcast(E2M1X4),
+                    lhsT_scale=ws[:, P * t : P * (t + 1)],
+                    rhs=codes[:].bitcast(E4M3X4),
+                    rhs_scale=scales[:],
+                    start=True,
+                    stop=True,
+                )
+                banks.append(bank)
+            return banks
+
+        y_ps = product(w1w, w1s, xw, xs, "A")
+        w2w = deal_words(w2w_raw, "w2w")
+        w2s = deal_scales(w2s_raw, "w2s")
+
+        def f32_tile(name, cols=S):
+            return sb.tile([P, cols], F32, name=name, align_bytes=64)
+
+        def weave(engine_copy, planes, cols, name, tag):
+            n = cols.stop - cols.start
+            woven = sb.tile([P, PACK * n], BF16, name=name, tag=tag, align_bytes=64)
+            engine_copy(
+                woven[:].rearrange("p (c i t) -> p c t i", t=PACK, i=4),
+                planes[:, :, cols].rearrange("p t (c i) -> p c t i", i=4),
+            )
+            return woven
+
+        def quantise(woven, name):
+            codes = sb.tile([P, S], U32, name=name + "_codes", align_bytes=64)
+            scales = sb.tile([P, S], U8, name=name + "_scales", align_bytes=64)
+            nc.vector.quantize_mx(out=codes[:].bitcast(E4M3X4), scales=scales[:], in_=woven[:])
+            return codes, scales
+
+        def evacuate(bank, name, win_scale, plain_scale):
+            win = f32_tile(name + "_win", 2 * S)
+            plain = f32_tile(name)
+            nc.scalar.activation(win[:, :S], bank[:], ACT.Copy, scale=win_scale)
+            nc.scalar.activation(plain[:], bank[:], ACT.Copy, scale=plain_scale)
+            return win, plain
+
+        everything = slice(0, S)
+        ny = [evacuate(y_ps[t], "ny%d" % t, -1.0, -1.0) for t in range(PACK)]
+        gy = [evacuate(y_ps[t], "gy%d" % t, gain34[:, t : t + 1], gain[:, t : t + 1]) for t in range(PACK)]
+
+        z2 = sb.tile([P, PACK, S], BF16, name="z2", align_bytes=64)
+        uv = []
+
+        def z2_finish(t):
+            m = f32_tile("m%d" % t)
+            nc.vector.tensor_tensor(m[:], uv[t][0][:], uv[t][1][:], ALU.max)
+            nc.scalar.activation(z2[:, t, :], m[:], ACT.Copy, scale=gain[:, t : t + 1])
+
+        for t in range(PACK):
+            win, plain = ny[t]
+            u = f32_tile("u%d" % t)
+            v = f32_tile("v%d" % t)
+            uv.append((u, v))
+            nc.vector.tensor_tensor(u[:], win[:].indirect(n3_t[:]), plain[:], ALU.subtract)
+            if t > 0:
+                z2_finish(t - 1)
+            nc.vector.tensor_tensor(v[:], win[:].indirect(n4_t[:]), plain[:], ALU.subtract)
+        part = []
+        for t in range(PACK):
+            win, plain = gy[t]
+            pt = f32_tile("part%d" % t)
+            nc.vector.tensor_tensor(pt[:], win[:].indirect(n1_t[:]), plain[:], ALU.subtract)
+            part.append(pt)
+            if t == 0:
+                z2_finish(PACK - 1)
+        z2_codes, z2_scales = quantise(weave(nc.scalar.copy, z2, everything, "z2_woven", "after_z2"), "z2")
+        b_ps = product(w2w, w2s, z2_codes, z2_scales, "B")
+        bb = [evacuate(b_ps[t], "b%d" % t, 1.0, 1.0) for t in range(PACK)]
+
+        z = sb.tile([P, PACK, S], F32, name="z", tag="after_z2", align_bytes=64)
+        for t in range(PACK):
+            nc.vector.tensor_tensor(z[:, t, :], gy[t][0][:].indirect(n2_t[:]), part[t][:], ALU.add)
+        z_codes, z_scales = quantise(weave(nc.scalar.copy, z, everything, "z_woven", "after_z"), "z")
+        a_ps = product(w2w, w2s, z_codes, z_scales, "A")
+
+        gate = []
+        aa = []
+        for t in range(PACK):
+            win, plain = bb[t]
+            db = sb.tile([P, S], F32, name="db%d" % t, tag="after_z" if t == PACK - 1 else "db%d" % t, align_bytes=64)
+            nc.vector.tensor_tensor(db[:], win[:].indirect(n6_t[:]), plain[:], ALU.subtract)
+            aa.append(evacuate(a_ps[t], "a%d" % t, 1.0, 1.0))
+            th = f32_tile("gate%d" % t)
+            nc.scalar.activation(th[:], db[:], ACT.Tanh, scale=0.5)
+            gate.append(th)
+
+        out_rows = out_0.rearrange("(p t) c -> p t c", t=PACK)
+        out_words = out_1[0].rearrange("p c r -> p (c r)").bitcast(I32)
+        o_scales = sb.tile([P, S], U8, name="o_scales", align_bytes=64)
+        res = sb.tile([P, PACK, S], F32, name="res", align_bytes=64)
+        halves = [slice(0, HALF), slice(HALF, S)]
+        pieces = [(0, everything), (1, everything), (2, halves[0]), (3, halves[0]), (2, halves[1]), (3, halves[1])]
+
+        def fetch(t, cols):
+            win, plain = aa[t]
+            da = f32_tile("da%d_%d" % (t, cols.start), cols.stop - cols.start)
+            nc.vector.tensor_tensor(
+                da[:], win[:].indirect(n5_t[:, cols.start // 16 : cols.stop // 16]), plain[:, cols], ALU.subtract
+            )
+            return da
+
+        def hand_on(h):
+            cols = halves[h]
+            woven = weave(nc.scalar.copy if h == 0 else nc.vector.tensor_copy, res, cols, "o_woven%d" % h, "o_woven%d" % h)
+            codes = sb.tile([P, HALF], I32, name="o_codes%d" % h, align_bytes=64)
+            nc.vector.quantize_mx(out=codes[:].bitcast(E4M3X4), scales=o_scales[:, cols], in_=woven[:])
+            nc.sync.dma_start(out_words[:, cols], codes[:])
+
+        da = fetch(*pieces[0])
+        for i, (t, cols) in enumerate(pieces):
+            pull = f32_tile("pull%d_%d" % (t, cols.start), cols.stop - cols.start)
+            nc.vector.scalar_tensor_tensor(pull[:], gate[t][:, cols], 1.0, da[:], ALU.add, ALU.mult)
+            if i + 1 < len(pieces):
+                da = fetch(*pieces[i + 1])
+            nc.vector.scalar_tensor_tensor(res[:, t, cols], pull[:], 0.5, aa[t][1][:, cols], ALU.mult, ALU.add)
+            nc.sync.dma_start(out_rows[:, t, cols], res[:, t, cols])
+        hand_on(0)
+        hand_on(1)
+        for q in range(4):
+            queue = nc.sync if q % 2 == 0 else nc.scalar
+            queue.dma_start(out_2[0, 4 * q : 4 * q + 4, :].bitcast(I32), o_scales[32 * q : 32 * q + 4, :].bitcast(I32))

@@ -36,31 +36,31 @@ def tile_picked_tiepullblapunder_none_po_kernel(
             nc.sync.dma_start(tl[:], src)
             return tl
 
-        def load_scale_rows(queue, dst, src):
+        def load_scale_rows(queues, dst, src):
             for q in range(4):
-                queue.dma_start(dst[32 * q : 32 * q + 4, :].bitcast(I32), src[0, 4 * q : 4 * q + 4, :].bitcast(I32))
+                queues[q].dma_start(dst[32 * q : 32 * q + 4, :].bitcast(I32), src[0, 4 * q : 4 * q + 4, :].bitcast(I32))
 
         xs_raw = sb.tile([P, T // 4], I32, name="xs_raw", align_bytes=64)
         w1s_raw = sb.tile([P, H // 4], I32, name="w1s_raw", align_bytes=64)
         w2s_raw = sb.tile([P, H // 4], I32, name="w2s_raw", align_bytes=64)
-        nc.gpsimd.memset(xs_raw[:], 0)
-        nc.gpsimd.memset(w1s_raw[:], 0)
+        nc.vector.memset(xs_raw[:], 0)
+        nc.vector.memset(w1s_raw[:], 0)
         nc.gpsimd.memset(w2s_raw[:], 0)
 
         offs_t = load_list(offs, "offs_t")
-        load_scale_rows(nc.scalar, xs_raw[:].bitcast(U8), x_scales)
-        xw_raw = sb.tile([P, T], I32, name="xw_raw", align_bytes=64)
-        nc.sync.dma_start(xw_raw[:], x_words[0].rearrange("p c r -> p (c r)").bitcast(I32))
         w1w_raw = sb.tile([P, H // 2], I32, name="w1w_raw", align_bytes=64)
         nc.sync.dma_start(w1w_raw[:], w1_words[0].bitcast(I32))
-        load_scale_rows(nc.sync, w1s_raw[:].bitcast(U8), w1_scales)
         n3_t = load_list(n3, "n3_t")
-        n4_t = load_list(n4, "n4_t")
+        xw_raw = sb.tile([P, T], I32, name="xw_raw", align_bytes=64)
+        nc.sync.dma_start(xw_raw[:], x_words[0].rearrange("p c r -> p (c r)").bitcast(I32))
+        load_scale_rows([nc.scalar] * 4, xs_raw[:].bitcast(U8), x_scales)
+        load_scale_rows([nc.sync, nc.sync, nc.gpsimd, nc.gpsimd], w1s_raw[:].bitcast(U8), w1_scales)
         gain = sb.tile([P, PACK], F32, name="gain")
-        nc.sync.dma_start(gain[:], gn.rearrange("(p t) o -> p (t o)", t=PACK))
+        nc.gpsimd.dma_start(gain[:], gn.rearrange("(p t) o -> p (t o)", t=PACK))
+        n4_t = load_list(n4, "n4_t")
         w2w_raw = sb.tile([P, H // 2], I32, name="w2w_raw", align_bytes=64)
         nc.sync.dma_start(w2w_raw[:], w2_words[0].bitcast(I32))
-        load_scale_rows(nc.sync, w2s_raw[:].bitcast(U8), w2_scales)
+        load_scale_rows([nc.sync] * 4, w2s_raw[:].bitcast(U8), w2_scales)
         n1_t = load_list(n1, "n1_t")
         n2_t = load_list(n2, "n2_t")
         n6_t = load_list(n6, "n6_t")
@@ -89,26 +89,28 @@ def tile_picked_tiepullblapunder_none_po_kernel(
         xs = sb.tile([P, S], U8, name="xs", align_bytes=64)
         nc.vector.tensor_copy(xs[:], xs_raw[:].bitcast(U8).indirect(offs_t[:]))
         w1s = deal_scales(w1s_raw, "w1s")
+        halves = [slice(0, HALF), slice(HALF, S)]
         xw = sb.tile([P, S], U32, name="xw", align_bytes=64)
-        nc.vector.tensor_copy(xw[:], xw_raw[:].bitcast(U32).indirect(offs_t[:]))
+        for cols in halves:
+            nc.vector.tensor_copy(xw[:, cols], xw_raw[:].bitcast(U32).indirect(offs_t[:, cols.start // 16 : cols.stop // 16]))
 
-        def product(ww, ws, codes, scales, tag):
-            banks = []
-            for t in range(PACK):
-                bank = ps.tile([P, S], F32, name="bank_%s%d" % (tag, t), tag="bank_%s%d" % (tag, t))
-                nc.tensor.matmul_mx(
-                    out=bank[:],
-                    lhsT=ww[:, 2 * P * t : 2 * P * (t + 1)].bitcast(E2M1X4),
-                    lhsT_scale=ws[:, P * t : P * (t + 1)],
-                    rhs=codes[:].bitcast(E4M3X4),
-                    rhs_scale=scales[:],
-                    start=True,
-                    stop=True,
-                )
-                banks.append(bank)
-            return banks
+        def product(ww, ws, codes, scales, t, cols, tag):
+            bank = ps.tile([P, cols.stop - cols.start], F32, name=tag, tag=tag)
+            nc.tensor.matmul_mx(
+                out=bank[:],
+                lhsT=ww[:, 2 * P * t : 2 * P * (t + 1)].bitcast(E2M1X4),
+                lhsT_scale=ws[:, P * t : P * (t + 1)],
+                rhs=codes[:, cols].bitcast(E4M3X4),
+                rhs_scale=scales[:, cols],
+                start=True,
+                stop=True,
+            )
+            return cols, bank
 
-        y_ps = product(w1w, w1s, xw, xs, "A")
+        everything = slice(0, S)
+        y_ps = [[product(w1w, w1s, xw, xs, 0, halves[0], "bank0"), product(w1w, w1s, xw, xs, 0, halves[1], "bank7")]]
+        for t in range(1, PACK):
+            y_ps.append([product(w1w, w1s, xw, xs, t, everything, "bank%d" % t)])
         w2w = deal_words(w2w_raw, "w2w")
         w2s = deal_scales(w2s_raw, "w2s")
 
@@ -130,14 +132,14 @@ def tile_picked_tiepullblapunder_none_po_kernel(
             nc.vector.quantize_mx(out=codes[:].bitcast(E4M3X4), scales=scales[:], in_=woven[:])
             return codes, scales
 
-        def evacuate(bank, name, win_scale, plain_scale):
+        def evacuate(banks, name, win_scale, plain_scale):
             win = f32_tile(name + "_win", 2 * S)
             plain = f32_tile(name)
-            nc.scalar.activation(win[:, :S], bank[:], ACT.Copy, scale=win_scale)
-            nc.scalar.activation(plain[:], bank[:], ACT.Copy, scale=plain_scale)
+            for cols, bank in banks:
+                nc.scalar.activation(win[:, cols], bank[:], ACT.Copy, scale=win_scale)
+                nc.scalar.activation(plain[:, cols], bank[:], ACT.Copy, scale=plain_scale)
             return win, plain
 
-        everything = slice(0, S)
         ny = [evacuate(y_ps[t], "ny%d" % t, -1.0, -1.0) for t in range(PACK)]
         gy = [evacuate(y_ps[t], "gy%d" % t, gain34[:, t : t + 1], gain[:, t : t + 1]) for t in range(PACK)]
 
@@ -167,31 +169,34 @@ def tile_picked_tiepullblapunder_none_po_kernel(
             if t == 0:
                 z2_finish(PACK - 1)
         z2_codes, z2_scales = quantise(weave(nc.scalar.copy, z2, everything, "z2_woven", "after_z2"), "z2")
-        b_ps = product(w2w, w2s, z2_codes, z2_scales, "B")
-        bb = [evacuate(b_ps[t], "b%d" % t, 1.0, 1.0) for t in range(PACK)]
+        b_ps = [[product(w2w, w2s, z2_codes, z2_scales, t, everything, "bank%d" % (PACK + t))] for t in range(PACK)]
+        bb = [evacuate(b_ps[t], "b%d" % t, 1.0, 1.0) for t in range(PACK - 1)]
 
         z = sb.tile([P, PACK, S], F32, name="z", tag="after_z2", align_bytes=64)
         for t in range(PACK):
             nc.vector.tensor_tensor(z[:, t, :], gy[t][0][:].indirect(n2_t[:]), part[t][:], ALU.add)
-        z_codes, z_scales = quantise(weave(nc.scalar.copy, z, everything, "z_woven", "after_z"), "z")
-        a_ps = product(w2w, w2s, z_codes, z_scales, "A")
+        z_woven = weave(nc.scalar.copy, z, everything, "z_woven", "after_z")
+        bb.append(evacuate(b_ps[PACK - 1], "b%d" % (PACK - 1), 1.0, 1.0))
+        z_codes, z_scales = quantise(z_woven, "z")
+        a_ps = [[product(w2w, w2s, z_codes, z_scales, t, everything, "bank%d" % t)] for t in range(PACK)]
 
         gate = []
         aa = []
+        db_early = sb.tile([P, 2, S], F32, name="db_early", align_bytes=64)
+        db_late = sb.tile([P, 2, S], F32, name="db_late", tag="after_z", align_bytes=64)
         for t in range(PACK):
             win, plain = bb[t]
-            db = sb.tile([P, S], F32, name="db%d" % t, tag="after_z" if t == PACK - 1 else "db%d" % t, align_bytes=64)
-            nc.vector.tensor_tensor(db[:], win[:].indirect(n6_t[:]), plain[:], ALU.subtract)
+            db = (db_early, db_late)[t // 2][:, t % 2, :]
+            nc.vector.tensor_tensor(db, win[:].indirect(n6_t[:]), plain[:], ALU.subtract)
             aa.append(evacuate(a_ps[t], "a%d" % t, 1.0, 1.0))
             th = f32_tile("gate%d" % t)
-            nc.scalar.activation(th[:], db[:], ACT.Tanh, scale=0.5)
+            nc.scalar.activation(th[:], db, ACT.Tanh, scale=0.5)
             gate.append(th)
 
         out_rows = out_0.rearrange("(p t) c -> p t c", t=PACK)
         out_words = out_1[0].rearrange("p c r -> p (c r)").bitcast(I32)
         o_scales = sb.tile([P, S], U8, name="o_scales", align_bytes=64)
         res = sb.tile([P, PACK, S], F32, name="res", align_bytes=64)
-        halves = [slice(0, HALF), slice(HALF, S)]
         pieces = [(0, everything), (1, everything), (2, halves[0]), (3, halves[0]), (2, halves[1]), (3, halves[1])]
 
         def fetch(t, cols):

@@ -55,8 +55,6 @@ def tile_picked_tiepullblapunder_none_po_kernel(
         nc.sync.dma_start(xw_raw[:], x_words[0].rearrange("p c r -> p (c r)").bitcast(I32))
         load_scale_rows([nc.scalar] * 4, xs_raw[:].bitcast(U8), x_scales)
         load_scale_rows([nc.sync, nc.sync, nc.gpsimd, nc.gpsimd], w1s_raw[:].bitcast(U8), w1_scales)
-        gain = sb.tile([P, PACK], F32, name="gain")
-        nc.gpsimd.dma_start(gain[:], gn.rearrange("(p t) o -> p (t o)", t=PACK))
         n4_t = load_list(n4, "n4_t")
         w2w_raw = sb.tile([P, H // 2], I32, name="w2w_raw", align_bytes=64)
         nc.sync.dma_start(w2w_raw[:], w2_words[0].bitcast(I32))
@@ -65,8 +63,6 @@ def tile_picked_tiepullblapunder_none_po_kernel(
         n2_t = load_list(n2, "n2_t")
         n6_t = load_list(n6, "n6_t")
         n5_t = load_list(n5, "n5_t")
-        gain34 = sb.tile([P, PACK], F32, name="gain34")
-        nc.gpsimd.tensor_scalar(gain34[:], gain[:], 0.75, 0.0, ALU.mult, ALU.add)
 
 
         def deal_words(raw, name):
@@ -86,6 +82,10 @@ def tile_picked_tiepullblapunder_none_po_kernel(
             return dealt
 
         w1w = deal_words(w1w_raw, "w1w")
+        gain = sb.tile([P, PACK], F32, name="gain", tag="w1w_raw", align_bytes=64)
+        nc.gpsimd.dma_start(gain[:], gn.rearrange("(p t) o -> p (t o)", t=PACK))
+        gain34 = sb.tile([P, PACK], F32, name="gain34")
+        nc.gpsimd.tensor_scalar(gain34[:], gain[:], 0.75, 0.0, ALU.mult, ALU.add)
         xs = sb.tile([P, S], U8, name="xs", align_bytes=64)
         nc.vector.tensor_copy(xs[:], xs_raw[:].bitcast(U8).indirect(offs_t[:]))
         w1s = deal_scales(w1s_raw, "w1s")
@@ -157,26 +157,38 @@ def tile_picked_tiepullblapunder_none_po_kernel(
             v = f32_tile("v%d" % t)
             uv.append((u, v))
             nc.vector.tensor_tensor(u[:], win[:].indirect(n3_t[:]), plain[:], ALU.subtract)
-            if t > 0:
+            if 0 < t < PACK - 1:
                 z2_finish(t - 1)
             nc.vector.tensor_tensor(v[:], win[:].indirect(n4_t[:]), plain[:], ALU.subtract)
+        z2_finish(PACK - 2)
+        z2_finish(PACK - 1)
         part = []
         for t in range(PACK):
             win, plain = gy[t]
             pt = f32_tile("part%d" % t)
             nc.vector.tensor_tensor(pt[:], win[:].indirect(n1_t[:]), plain[:], ALU.subtract)
             part.append(pt)
-            if t == 0:
-                z2_finish(PACK - 1)
         z2_codes, z2_scales = quantise(weave(nc.scalar.copy, z2, everything, "z2_woven", "after_z2"), "z2")
         b_ps = [[product(w2w, w2s, z2_codes, z2_scales, t, everything, "bank%d" % (PACK + t))] for t in range(PACK)]
-        bb = [evacuate(b_ps[t], "b%d" % t, 1.0, 1.0) for t in range(PACK - 1)]
+        bb = []
+        for t in range(PACK):
+            win = f32_tile("b%d_win" % t, 2 * S)
+            plain = f32_tile("b%d" % t)
+            nc.scalar.copy(win[:, everything], b_ps[t][0][1][:])
+            nc.sync.dma_start(plain[:], win[:, everything])
+            bb.append((win, plain))
 
         z = sb.tile([P, PACK, S], F32, name="z", tag="after_z2", align_bytes=64)
-        for t in range(PACK):
-            nc.vector.tensor_tensor(z[:, t, :], gy[t][0][:].indirect(n2_t[:]), part[t][:], ALU.add)
-        z_woven = weave(nc.scalar.copy, z, everything, "z_woven", "after_z")
-        bb.append(evacuate(b_ps[PACK - 1], "b%d" % (PACK - 1), 1.0, 1.0))
+        pieces = [(0, everything), (1, everything), (2, halves[0]), (3, halves[0]), (2, halves[1]), (3, halves[1])]
+        for t, cols in pieces:
+            places = n2_t[:, cols.start // 16 : cols.stop // 16]
+            nc.vector.tensor_tensor(z[:, t, cols], gy[t][0][:].indirect(places), part[t][:, cols], ALU.add)
+        z_woven = sb.tile([P, PACK * S], BF16, name="z_woven", tag="after_z", align_bytes=64)
+        for cols in halves:
+            nc.scalar.copy(
+                z_woven[:, PACK * cols.start : PACK * cols.stop].rearrange("p (c i t) -> p c t i", t=PACK, i=4),
+                z[:, :, cols].rearrange("p t (c i) -> p c t i", i=4),
+            )
         z_codes, z_scales = quantise(z_woven, "z")
         a_ps = [[product(w2w, w2s, z_codes, z_scales, t, everything, "bank%d" % t)] for t in range(PACK)]
 
@@ -197,7 +209,6 @@ def tile_picked_tiepullblapunder_none_po_kernel(
         out_words = out_1[0].rearrange("p c r -> p (c r)").bitcast(I32)
         o_scales = sb.tile([P, S], U8, name="o_scales", align_bytes=64)
         res = sb.tile([P, PACK, S], F32, name="res", align_bytes=64)
-        pieces = [(0, everything), (1, everything), (2, halves[0]), (3, halves[0]), (2, halves[1]), (3, halves[1])]
 
         def fetch(t, cols):
             win, plain = aa[t]

from contextlib import ExitStack

import concourse.mybir as mybir

F32 = mybir.dt.float32
BF16 = mybir.dt.bfloat16
I32 = mybir.dt.int32
U32 = mybir.dt.uint32
U16 = mybir.dt.uint16
U8 = mybir.dt.uint8
E4M3X4 = mybir.dt.float8_e4m3fn_x4
E2M1X4 = mybir.dt.float4_e2m1fn_x4
ALU = mybir.AluOpType
ACT = mybir.ActivationFunctionType

P = 128
PACK = 4
T = 2048
S = 512
H = 512
HALF = S // 2
FLOPS = 3 * 2 * 512 * 512 * 512


def tile_picked_tiepullblapunder_none_po_kernel(
    tc, x_words, x_scales, w1_words, w1_scales, gn, w2_words, w2_scales, offs, n1, n2, n3, n4, n5, n6, out_0, out_1, out_2
):
    nc = tc.nc
    with ExitStack() as ctx:
        lists = ctx.enter_context(tc.tile_pool(name="lists", bufs=1))
        sb = ctx.enter_context(tc.tile_pool(name="sb", bufs=1))
        ps = ctx.enter_context(tc.psum_pool(name="ps", bufs=1))

        def load_list(src, name):
            tl = lists.tile([P, S // 16], U16, name=name)
            nc.sync.dma_start(tl[:], src)
            return tl

        def load_scale_rows(queues, dst, src):
            for q in range(4):
                queues[q].dma_start(dst[32 * q : 32 * q + 4, :].bitcast(I32), src[0, 4 * q : 4 * q + 4, :].bitcast(I32))

        xs_raw = sb.tile([P, T // 4], I32, name="xs_raw", align_bytes=64)
        w1s_raw = sb.tile([P, H // 4], I32, name="w1s_raw", align_bytes=64)
        w2s_raw = sb.tile([P, H // 4], I32, name="w2s_raw", align_bytes=64)
        nc.vector.memset(xs_raw[:], 0)
        nc.vector.memset(w1s_raw[:], 0)
        nc.gpsimd.memset(w2s_raw[:], 0)

        offs_t = load_list(offs, "offs_t")
        w1w_raw = sb.tile([P, H // 2], I32, name="w1w_raw", align_bytes=64)
        nc.sync.dma_start(w1w_raw[:], w1_words[0].bitcast(I32))
        n3_t = load_list(n3, "n3_t")
        xw_raw = sb.tile([P, T], I32, name="xw_raw", align_bytes=64)
        nc.sync.dma_start(xw_raw[:], x_words[0].rearrange("p c r -> p (c r)").bitcast(I32))
        load_scale_rows([nc.scalar] * 4, xs_raw[:].bitcast(U8), x_scales)
        load_scale_rows([nc.sync, nc.sync, nc.gpsimd, nc.gpsimd], w1s_raw[:].bitcast(U8), w1_scales)
        n4_t = load_list(n4, "n4_t")
        w2w_raw = sb.tile([P, H // 2], I32, name="w2w_raw", align_bytes=64)
        nc.sync.dma_start(w2w_raw[:], w2_words[0].bitcast(I32))
        load_scale_rows([nc.sync] * 4, w2s_raw[:].bitcast(U8), w2_scales)
        n1_t = load_list(n1, "n1_t")
        n2_t = load_list(n2, "n2_t")
        n6_t = load_list(n6, "n6_t")
        n5_t = load_list(n5, "n5_t")


        def deal_words(raw, name):
            dealt = sb.tile([P, 2 * H], U8, name=name, align_bytes=64)
            nc.vector.tensor_copy(
                dealt[:].rearrange("p (t m b) -> p t m b", t=PACK, b=2),
                raw[:].bitcast(U8).rearrange("p (m t b) -> p t m b", t=PACK, b=2),
            )
            return dealt

        def deal_scales(raw, name):
            dealt = sb.tile([P, H], U8, name=name, align_bytes=64)
            nc.vector.tensor_copy(
                dealt[:].rearrange("p (t m) -> p t m", t=PACK),
                raw[:].bitcast(U8).rearrange("p (m t) -> p t m", t=PACK),
            )
            return dealt

        w1w = deal_words(w1w_raw, "w1w")
        gain = sb.tile([P, PACK], F32, name="gain", tag="w1w_raw", align_bytes=64)
        nc.gpsimd.dma_start(gain[:], gn.rearrange("(p t) o -> p (t o)", t=PACK))
        gain34 = sb.tile([P, PACK], F32, name="gain34")
        nc.gpsimd.tensor_scalar(gain34[:], gain[:], 0.75, 0.0, ALU.mult, ALU.add)
        xs = sb.tile([P, S], U8, name="xs", align_bytes=64)
        nc.vector.tensor_copy(xs[:], xs_raw[:].bitcast(U8).indirect(offs_t[:]))
        w1s = deal_scales(w1s_raw, "w1s")
        halves = [slice(0, HALF), slice(HALF, S)]
        xw = sb.tile([P, S], U32, name="xw", align_bytes=64)
        for cols in halves:
            nc.vector.tensor_copy(xw[:, cols], xw_raw[:].bitcast(U32).indirect(offs_t[:, cols.start // 16 : cols.stop // 16]))

        def product(ww, ws, codes, scales, t, cols, tag):
            bank = ps.tile([P, cols.stop - cols.start], F32, name=tag, tag=tag)
            nc.tensor.matmul_mx(
                out=bank[:],
                lhsT=ww[:, 2 * P * t : 2 * P * (t + 1)].bitcast(E2M1X4),
                lhsT_scale=ws[:, P * t : P * (t + 1)],
                rhs=codes[:, cols].bitcast(E4M3X4),
                rhs_scale=scales[:, cols],
                start=True,
                stop=True,
            )
            return cols, bank

        everything = slice(0, S)
        y_ps = [[product(w1w, w1s, xw, xs, 0, halves[0], "bank0"), product(w1w, w1s, xw, xs, 0, halves[1], "bank7")]]
        for t in range(1, PACK):
            y_ps.append([product(w1w, w1s, xw, xs, t, everything, "bank%d" % t)])
        w2w = deal_words(w2w_raw, "w2w")
        w2s = deal_scales(w2s_raw, "w2s")

        def f32_tile(name, cols=S):
            return sb.tile([P, cols], F32, name=name, align_bytes=64)

        def weave(engine_copy, planes, cols, name, tag):
            n = cols.stop - cols.start
            woven = sb.tile([P, PACK * n], BF16, name=name, tag=tag, align_bytes=64)
            engine_copy(
                woven[:].rearrange("p (c i t) -> p c t i", t=PACK, i=4),
                planes[:, :, cols].rearrange("p t (c i) -> p c t i", i=4),
            )
            return woven

        def quantise(woven, name):
            codes = sb.tile([P, S], U32, name=name + "_codes", align_bytes=64)
            scales = sb.tile([P, S], U8, name=name + "_scales", align_bytes=64)
            nc.vector.quantize_mx(out=codes[:].bitcast(E4M3X4), scales=scales[:], in_=woven[:])
            return codes, scales

        def evacuate(banks, name, win_scale, plain_scale):
            win = f32_tile(name + "_win", 2 * S)
            plain = f32_tile(name)
            for cols, bank in banks:
                nc.scalar.activation(win[:, cols], bank[:], ACT.Copy, scale=win_scale)
                nc.scalar.activation(plain[:, cols], bank[:], ACT.Copy, scale=plain_scale)
            return win, plain

        ny = [evacuate(y_ps[t], "ny%d" % t, -1.0, -1.0) for t in range(PACK)]
        gy = [evacuate(y_ps[t], "gy%d" % t, gain34[:, t : t + 1], gain[:, t : t + 1]) for t in range(PACK)]

        z2 = sb.tile([P, PACK, S], BF16, name="z2", align_bytes=64)
        uv = []

        def z2_finish(t):
            m = f32_tile("m%d" % t)
            nc.vector.tensor_tensor(m[:], uv[t][0][:], uv[t][1][:], ALU.max)
            nc.scalar.activation(z2[:, t, :], m[:], ACT.Copy, scale=gain[:, t : t + 1])

        for t in range(PACK):
            win, plain = ny[t]
            u = f32_tile("u%d" % t)
            v = f32_tile("v%d" % t)
            uv.append((u, v))
            nc.vector.tensor_tensor(u[:], win[:].indirect(n3_t[:]), plain[:], ALU.subtract)
            if 0 < t < PACK - 1:
                z2_finish(t - 1)
            nc.vector.tensor_tensor(v[:], win[:].indirect(n4_t[:]), plain[:], ALU.subtract)
        z2_finish(PACK - 2)
        z2_finish(PACK - 1)
        part = []
        for t in range(PACK):
            win, plain = gy[t]
            pt = f32_tile("part%d" % t)
            nc.vector.tensor_tensor(pt[:], win[:].indirect(n1_t[:]), plain[:], ALU.subtract)
            part.append(pt)
        z2_codes, z2_scales = quantise(weave(nc.scalar.copy, z2, everything, "z2_woven", "after_z2"), "z2")
        b_ps = [[product(w2w, w2s, z2_codes, z2_scales, t, everything, "bank%d" % (PACK + t))] for t in range(PACK)]
        bb = []
        for t in range(PACK):
            win = f32_tile("b%d_win" % t, 2 * S)
            plain = f32_tile("b%d" % t)
            nc.scalar.copy(win[:, everything], b_ps[t][0][1][:])
            nc.sync.dma_start(plain[:], win[:, everything])
            bb.append((win, plain))

        z = sb.tile([P, PACK, S], F32, name="z", tag="after_z2", align_bytes=64)
        pieces = [(0, everything), (1, everything), (2, halves[0]), (3, halves[0]), (2, halves[1]), (3, halves[1])]
        for t, cols in pieces:
            places = n2_t[:, cols.start // 16 : cols.stop // 16]
            nc.vector.tensor_tensor(z[:, t, cols], gy[t][0][:].indirect(places), part[t][:, cols], ALU.add)
        z_woven = sb.tile([P, PACK * S], BF16, name="z_woven", tag="after_z", align_bytes=64)
        for cols in halves:
            nc.scalar.copy(
                z_woven[:, PACK * cols.start : PACK * cols.stop].rearrange("p (c i t) -> p c t i", t=PACK, i=4),
                z[:, :, cols].rearrange("p t (c i) -> p c t i", i=4),
            )
        z_codes, z_scales = quantise(z_woven, "z")
        a_ps = [[product(w2w, w2s, z_codes, z_scales, t, everything, "bank%d" % t)] for t in range(PACK)]

        gate = []
        aa = []
        db_early = sb.tile([P, 2, S], F32, name="db_early", align_bytes=64)
        db_late = sb.tile([P, 2, S], F32, name="db_late", tag="after_z", align_bytes=64)
        for t in range(PACK):
            win, plain = bb[t]
            db = (db_early, db_late)[t // 2][:, t % 2, :]
            nc.vector.tensor_tensor(db, win[:].indirect(n6_t[:]), plain[:], ALU.subtract)
            aa.append(evacuate(a_ps[t], "a%d" % t, 1.0, 1.0))
            th = f32_tile("gate%d" % t)
            nc.scalar.activation(th[:], db, ACT.Tanh, scale=0.5)
            gate.append(th)

        out_rows = out_0.rearrange("(p t) c -> p t c", t=PACK)
        out_words = out_1[0].rearrange("p c r -> p (c r)").bitcast(I32)
        o_scales = sb.tile([P, S], U8, name="o_scales", align_bytes=64)
        res = sb.tile([P, PACK, S], F32, name="res", align_bytes=64)

        def fetch(t, cols):
            win, plain = aa[t]
            da = f32_tile("da%d_%d" % (t, cols.start), cols.stop - cols.start)
            nc.vector.tensor_tensor(
                da[:], win[:].indirect(n5_t[:, cols.start // 16 : cols.stop // 16]), plain[:, cols], ALU.subtract
            )
            return da

        def hand_on(h):
            cols = halves[h]
            woven = weave(nc.scalar.copy if h == 0 else nc.vector.tensor_copy, res, cols, "o_woven%d" % h, "o_woven%d" % h)
            codes = sb.tile([P, HALF], I32, name="o_codes%d" % h, align_bytes=64)
            nc.vector.quantize_mx(out=codes[:].bitcast(E4M3X4), scales=o_scales[:, cols], in_=woven[:])
            nc.sync.dma_start(out_words[:, cols], codes[:])

        da = fetch(*pieces[0])
        for i, (t, cols) in enumerate(pieces):
            pull = f32_tile("pull%d_%d" % (t, cols.start), cols.stop - cols.start)
            nc.vector.scalar_tensor_tensor(pull[:], gate[t][:, cols], 1.0, da[:], ALU.add, ALU.mult)
            if i + 1 < len(pieces):
                da = fetch(*pieces[i + 1])
            nc.vector.scalar_tensor_tensor(res[:, t, cols], pull[:], 0.5, aa[t][1][:, cols], ALU.mult, ALU.add)
            nc.sync.dma_start(out_rows[:, t, cols], res[:, t, cols])
        hand_on(0)
        hand_on(1)
        for q in range(4):
            queue = nc.sync if q % 2 == 0 else nc.scalar
            queue.dma_start(out_2[0, 4 * q : 4 * q + 4, :].bitcast(I32), o_scales[32 * q : 32 * q + 4, :].bitcast(I32))
